import numpy as np
import ml_dtypes


def mxq(x, axis, fmt="e4m3"):
    dtype, down = {"e4m3": (ml_dtypes.float8_e4m3fn, 7), "e5m2": (ml_dtypes.float8_e5m2, 14)}[fmt]
    v = np.moveaxis(np.asarray(x, np.float32).astype(ml_dtypes.bfloat16).astype(np.float64), axis, -1)
    blocks = v.reshape(v.shape[:-1] + (-1, 32))
    amax = np.abs(blocks).max(-1, keepdims=True)
    byte = np.maximum(np.where(amax > 0, np.frexp(amax)[1] - 1 + 127, 0) - down, 1)
    scale = np.exp2(byte - 127.0)
    codes = (blocks / scale).astype(np.float32).astype(dtype).astype(np.float64)
    return np.moveaxis((codes * scale).reshape(v.shape), -1, axis)


WIDE = False


def mx_kscale(k):
    if not WIDE:
        return np.ones(k)
    levels = np.array([10, -10, 5, -5, 0])
    if k % 512:
        return np.exp2(np.random.permutation(np.resize(levels, k // 32))).repeat(32)
    a = np.empty((k // 512, 16))
    for p in range(k // 512):
        a[p, :8] = np.random.permutation(np.resize(levels, 8))
        for g in range(8):
            far = levels[np.abs(levels - a[p, g]) >= 10]
            a[p, g + 8] = far[np.random.randint(len(far))]
    return np.exp2(a.ravel()).repeat(32)


def f64(x):
    return np.asarray(x).astype(np.float64)


def striped(idx):
    return np.tile(idx.reshape(-1, 16).T, (8, 1)).astype(np.uint16)


def unstriped(offs):
    return offs[:16].T.reshape(-1).astype(np.int64)


def striped8(idx):
    return np.concatenate([x.reshape(-1, 16).T for x in idx]).astype(np.uint16)


def runs(offs, k):
    lists = np.stack([offs[16 * r : 16 * r + 16].T.reshape(-1) for r in range(8)]).astype(np.int64)
    return lists[np.arange(k) % 512 // 64]


def pack_weight(w):
    k, n = w.shape
    w = f64(np.asarray(w, np.float32).astype(ml_dtypes.bfloat16)).reshape(k // 32, 32, n)
    amax = np.abs(w).max(1)
    byte = np.clip(np.where(amax > 0, np.frexp(amax)[1] - 1 + 127 - 7, 1), 1, 254)
    scaled = (w * np.exp2(127.0 - byte)[:, None, :]).reshape(k, n).astype(np.float32)
    words = np.ascontiguousarray(scaled.reshape(k // 512, 128, 4, n).transpose(0, 1, 3, 2)).astype(ml_dtypes.float8_e4m3fn).view(np.uint8)
    return words, np.ascontiguousarray(byte.astype(np.uint8).reshape(k // 512, 16, n))


def unpack_weight(words, scales):
    g, p, n, _ = words.shape
    vals = np.ascontiguousarray(words).view(ml_dtypes.float8_e4m3fn).astype(np.float64) * np.repeat(np.exp2(scales.astype(np.float64) - 127.0), 8, axis=1)[..., None]
    return vals.transpose(0, 1, 3, 2).reshape(g * 512, n)


E2M1 = np.array([0.0, 0.5, 1.0, 1.5, 2.0, 3.0, 4.0, 6.0, -0.0, -0.5, -1.0, -1.5, -2.0, -3.0, -4.0, -6.0])


def pack_fp4(w):
    k, n = w.shape
    w = f64(np.asarray(w, np.float32).astype(ml_dtypes.bfloat16)).reshape(k // 32, 32, n)
    amax = np.abs(w).max(1)
    mant, ex = np.frexp(amax / 6.0)
    byte = np.clip(np.where(amax > 0, np.where(mant > 0.5, ex, ex - 1) + 127, 1), 1, 254)
    scaled = (w * np.exp2(127.0 - byte)[:, None, :]).reshape(k, n).astype(np.float32)
    c = np.ascontiguousarray(scaled.reshape(k // 512, 128, 4, n).transpose(0, 1, 3, 2)).astype(ml_dtypes.float4_e2m1fn).view(np.uint8) & 0xF
    words = (c[..., 0::2] | (c[..., 1::2] << 4)).reshape(k // 512, 128, 2 * n)
    return np.ascontiguousarray(words), np.ascontiguousarray(byte.astype(np.uint8).reshape(k // 512, 16, n))


def unpack_fp4(words, scales):
    g, _, n = scales.shape
    words = np.ascontiguousarray(words).reshape(g, 128, n, 2)
    nib = np.empty((g, 128, n, 4), np.uint8)
    nib[..., 0::2] = words & 0xF
    nib[..., 1::2] = words >> 4
    vals = E2M1[nib] * np.repeat(np.exp2(scales.astype(np.float64) - 127.0), 8, axis=1)[..., None]
    return vals.transpose(0, 1, 3, 2).reshape(g * 512, n)


def sigmoid(v):
    return 1.0 / (1.0 + np.exp(-np.maximum(v, -700.0)))

def planes(y):
    n, m = y.shape
    v = y.astype(np.float32).astype(ml_dtypes.bfloat16).astype(np.float64).reshape(n // 32, 32, m)
    top = np.abs(v).max(1)
    byte = np.clip(np.where(top > 0, np.frexp(top)[1] - 1 + 127 - 7, 1), 1, 254)
    codes = (v * np.exp2(127.0 - byte)[:, None, :]).reshape(n, m).astype(np.float32).astype(ml_dtypes.float8_e4m3fn).view(np.uint8)
    words = codes.reshape(n // 512, 128, 4, m).transpose(0, 1, 3, 2)
    return np.ascontiguousarray(words), np.ascontiguousarray(byte.astype(np.uint8).reshape(n // 512, 16, m))


K, T, S, H, W, C = 512, 2048, 256, 512, 128, 512


def setup_inputs():
    n = np.random.standard_normal
    s = mx_kscale(K)[:, None]
    packed_xT = pack_weight(n((K, T)) * s)
    packed_w1 = pack_fp4(n((K, H)) / np.sqrt(K) / s)
    perm = np.random.permutation(S)
    return {
        "x_words": packed_xT[0],
        "x_scales": packed_xT[1],
        "w1_words": packed_w1[0],
        "w1_scales": packed_w1[1],
        "gs": (np.random.uniform(0.5, 1.5, (K, 1)) / s).astype(np.float32),
        "offs": striped8(np.random.randint(0, T, (8, S))),
        "n1": striped(perm[:W]),
        "n2": striped(perm[W:]),
        "cand": striped8(np.random.randint(0, T, (8, C))),
        "n3": striped8(np.stack([np.random.permutation(S) for _ in range(8)])),
        "n4": striped8(np.stack([np.random.permutation(S) for _ in range(8)])),
    }


def reference(x_words, x_scales, w1_words, w1_scales, gs, offs, n1, n2, cand, n3, n4):
    x_cand = unpack_weight(x_words, x_scales)[np.arange(K)[:, None], runs(cand, K)]
    xq = unpack_weight(x_words, x_scales)[np.arange(K)[:, None], runs(offs, K)]
    y = unpack_fp4(w1_words, w1_scales).T @ xq
    pa = y[:, unstriped(n1)]
    pb = y[:, unstriped(n2)]
    rb = np.minimum(pa, pb)
    ra = np.maximum(pa, pb)
    ds = np.zeros((H, S))
    ds[:, unstriped(n1)] = ra
    dt = ds.copy()
    dt[:, unstriped(n2)] = rb
    z = f64(gs) * dt
    s = 0.0625 * ((x_cand.T @ mxq(z, 0, "e4m3")))
    out_0 = (s - (s[np.arange(C)[:, None], runs(n3, C)])) * (sigmoid(s[np.arange(C)[:, None], runs(n4, C)]))
    return (out_0,) + planes(out_0)

@@ -1,0 +1,206 @@
+from contextlib import ExitStack
+
+import concourse.mybir as mybir
+
+K, T, S, H, W, C = 512, 2048, 256, 512, 128, 512
+FLOPS = 2 * K * H * S + 2 * K * C * S
+
+F32 = mybir.dt.float32
+BF16 = mybir.dt.bfloat16
+I32 = mybir.dt.int32
+U32 = mybir.dt.uint32
+U16 = mybir.dt.uint16
+U8 = mybir.dt.uint8
+FP8X4 = mybir.dt.float8_e4m3fn_x4
+FP4X4 = mybir.dt.float4_e2m1fn_x4
+ALU = mybir.AluOpType
+ACT = mybir.ActivationFunctionType
+
+P = 128
+PACK = 4
+
+
+def tile_picked_hcandordergdif_none_po_kernel(
+    tc, x_words, x_scales, w1_words, w1_scales, gs, offs, n1, n2, cand, n3, n4, out_0, out_1, out_2
+):
+    nc = tc.nc
+    with ExitStack() as ctx:
+        lists = ctx.enter_context(tc.tile_pool(name="lists", bufs=1))
+        keep = ctx.enter_context(tc.tile_pool(name="keep", bufs=1))
+        psum = ctx.enter_context(tc.psum_pool(name="psum", bufs=1))
+
+        offs_t = lists.tile([P, S // 16], U16, name="offs_t")
+        cand_t = lists.tile([P, C // 16], U16, name="cand_t")
+        n1_t = lists.tile([P, W // 16], U16, name="n1_t")
+        n2_t = lists.tile([P, W // 16], U16, name="n2_t")
+        n3_t = lists.tile([P, S // 16], U16, name="n3_t")
+        n4_t = lists.tile([P, S // 16], U16, name="n4_t")
+
+        table_words = keep.tile([P, T], U32, name="table_words", align_bytes=64)
+        table_scales = keep.tile([P, T], U8, name="table_scales", align_bytes=64)
+        w1_raw = keep.tile([P, 2 * H], U8, name="w1_raw", align_bytes=64)
+        w1_scales_raw = keep.tile([P, H], U8, name="w1_scales_raw", align_bytes=64)
+        w1_dealt = keep.tile([P, 2 * H], U8, name="w1_dealt", align_bytes=64)
+        w1_scales_dealt = keep.tile([P, H], U8, name="w1_scales_dealt", align_bytes=64)
+        gs_t = keep.tile([P, PACK], F32, name="gs_t")
+        place_words = keep.tile([P, S], U32, name="place_words", align_bytes=64)
+        place_bytes = keep.tile([P, S], U8, name="place_bytes", align_bytes=64)
+        place_scales = keep.tile([P, S], U8, name="place_scales", align_bytes=64)
+        cand_words_dealt = keep.tile([P, C], U32, name="cand_words_dealt", align_bytes=64)
+        cand_scales = keep.tile([P, C], U8, name="cand_scales", align_bytes=64)
+        cand_scales_dealt = keep.tile([P, C], U8, name="cand_scales_dealt", align_bytes=64)
+
+        nc.gpsimd.memset(w1_scales_raw[:].bitcast(I32), 0)
+        nc.gpsimd.memset(place_scales[:].bitcast(I32), 0)
+        nc.gpsimd.memset(cand_scales[:].bitcast(I32), 0)
+
+        nc.sync.dma_start(offs_t[:], offs)
+        nc.scalar.dma_start(w1_raw[:].bitcast(I32), w1_words[0].bitcast(I32))
+        nc.sync.dma_start(
+            table_scales[:].bitcast(I32), x_scales[0].bitcast(I32).unsqueeze(1).broadcast_to([16, 8, T // 4])
+        )
+        for q in range(4):
+            nc.scalar.dma_start(
+                w1_scales_raw[32 * q : 32 * q + 4, :].bitcast(I32), w1_scales[0, 4 * q : 4 * q + 4, :].bitcast(I32)
+            )
+        nc.sync.dma_start(table_words[:].bitcast(I32), x_words[0].rearrange("p c r -> p (c r)").bitcast(I32))
+        nc.sync.dma_start(n1_t[:], n1)
+        nc.sync.dma_start(n2_t[:], n2)
+        nc.sync.dma_start(cand_t[:], cand)
+
+        def place_scale_rows(dst, src, queues):
+            for j in range(4):
+                queues[j % len(queues)].dma_start(dst[j:P:32, :].bitcast(I32), src[8 * j : P : 32, :].bitcast(I32))
+
+        nc.vector.tensor_copy(place_bytes[:], table_scales[:].indirect(offs_t[:]))
+        place_scale_rows(place_scales, place_bytes, [nc.sync, nc.scalar])
+        nc.sync.dma_start(gs_t[:], gs.rearrange("(p t) o -> p (t o)", t=PACK))
+        nc.sync.dma_start(n3_t[:], n3)
+        nc.sync.dma_start(n4_t[:], n4)
+
+        nc.vector.tensor_copy(
+            w1_dealt[:].rearrange("p (t m b) -> p t m b", t=PACK, b=2),
+            w1_raw[:].rearrange("p (m t b) -> p t m b", t=PACK, b=2),
+        )
+        nc.vector.tensor_copy(
+            w1_scales_dealt[:].rearrange("p (t m) -> p t m", t=PACK),
+            w1_scales_raw[:].rearrange("p (m t) -> p t m", t=PACK),
+        )
+        nc.vector.tensor_copy(place_words[:], table_words[:].indirect(offs_t[:]))
+
+        y_sb, larger, smaller = [], [], []
+        for t in range(PACK):
+            y_ps = psum.tile([P, S], F32, name="y_ps", tag="bank%d" % t)
+            nc.tensor.matmul_mx(
+                out=y_ps[:],
+                lhsT=w1_dealt[:, 2 * P * t : 2 * P * (t + 1)].bitcast(FP4X4),
+                lhsT_scale=w1_scales_dealt[:, P * t : P * (t + 1)],
+                rhs=place_words[:].bitcast(FP8X4),
+                rhs_scale=place_scales[:],
+                start=True,
+                stop=True,
+            )
+            y_t = keep.tile([P, S], F32, name="y%d" % t)
+            nc.vector.tensor_copy(y_t[:], y_ps[:])
+            y_sb.append(y_t)
+
+        z_bf = keep.tile([P, S, PACK], BF16, name="z_bf", align_bytes=64)
+
+        for t in range(PACK):
+            pa = keep.tile([P, W], F32, name="pa%d" % t, tag="pa%d" % t, align_bytes=64)
+            pb = keep.tile([P, W], F32, name="pb%d" % t)
+            nc.scalar.activation(pa[:], y_sb[t][:].indirect(n1_t[:]), ACT.Copy)
+            nc.scalar.activation(pb[:], y_sb[t][:].indirect(n2_t[:]), ACT.Copy)
+            ra = keep.tile([P, W], F32, name="ra%d" % t)
+            rb = keep.tile([P, W], F32, name="rb%d" % t)
+            nc.vector.tensor_tensor(ra[:], pa[:], pb[:], ALU.max)
+            nc.vector.tensor_tensor(rb[:], pa[:], pb[:], ALU.min)
+            larger.append(ra)
+            smaller.append(rb)
+
+        cand_bytes = keep.tile([P, C], U8, name="cand_bytes", tag="pa1", align_bytes=64)
+        nc.vector.tensor_copy(cand_bytes[:], table_scales[:].indirect(cand_t[:]))
+        place_scale_rows(cand_scales, cand_bytes, [nc.sync])
+        cand_words = keep.tile([P, C], U32, name="cand_words", tag="pa3", align_bytes=64)
+        nc.vector.tensor_copy(cand_words[:], table_words[:].indirect(cand_t[:]))
+        nc.vector.tensor_copy(
+            cand_words_dealt[:].bitcast(I32).rearrange("p (t m) -> p t m", t=PACK),
+            cand_words[:].bitcast(I32).rearrange("p (m t) -> p t m", t=PACK),
+        )
+        nc.vector.tensor_copy(
+            cand_scales_dealt[:].rearrange("p (t m) -> p t m", t=PACK),
+            cand_scales[:].rearrange("p (m t) -> p t m", t=PACK),
+        )
+
+        dt = [keep.tile([P, S], F32, name="dt%d" % t) for t in range(PACK)]
+        for pair in range(2):
+            for t in (2 * pair, 2 * pair + 1):
+                nc.scalar.activation(dt[t][:].indirect(n1_t[:]), larger[t][:], ACT.Copy)
+            for t in (2 * pair, 2 * pair + 1):
+                nc.scalar.activation(dt[t][:].indirect(n2_t[:]), smaller[t][:], ACT.Copy)
+        halves = [slice(0, S // 2), slice(S // 2, S)]
+        for t in range(PACK - 1):
+            nc.vector.tensor_scalar(z_bf[:, :, t], dt[t][:], gs_t[:, t : t + 1], None, ALU.mult)
+        last = PACK - 1
+        for cols in halves:
+            nc.vector.tensor_scalar(z_bf[:, cols, last], dt[last][:, cols], gs_t[:, last:PACK], None, ALU.mult)
+
+        z_words = keep.tile([P, S], U32, name="z_words", align_bytes=64)
+        z_scales = keep.tile([P, S], U8, name="z_scales", align_bytes=64)
+        for cols in halves:
+            nc.vector.quantize_mx(
+                out=z_words[:, cols].bitcast(FP8X4),
+                scales=z_scales[:, cols],
+                in_=z_bf[:, cols, :].rearrange("p j t -> p (j t)"),
+            )
+
+        s_sb = [keep.tile([P, 2 * S], F32, name="s%d" % t) for t in range(PACK)]
+
+        def score(t, cols, bank):
+            s_ps = psum.tile([P, cols.stop - cols.start], F32, name="s_ps", tag=bank)
+            nc.tensor.matmul_mx(
+                out=s_ps[:],
+                lhsT=cand_words_dealt[:, P * t : P * (t + 1)].bitcast(FP8X4),
+                lhsT_scale=cand_scales_dealt[:, P * t : P * (t + 1)],
+                rhs=z_words[:, cols].bitcast(FP8X4),
+                rhs_scale=z_scales[:, cols],
+                start=True,
+                stop=True,
+            )
+            nc.vector.tensor_scalar(s_sb[t][:, cols], s_ps[:], 0.0625, None, ALU.mult)
+
+        score(0, halves[0], "bank0")
+        score(0, halves[1], "bank4")
+        for t in range(1, PACK):
+            score(t, slice(0, S), "bank%d" % (4 + t))
+
+        out_rows = out_0.rearrange("(p t) j -> p t j", t=PACK)
+        out_bf = keep.tile([P, S, PACK], BF16, name="out_bf", align_bytes=64)
+        for half in range(2):
+            res = keep.tile([P, 2, S], F32, name="res%d" % half)
+            for u in range(2):
+                t = 2 * half + u
+                other = keep.tile([P, S], F32, name="other%d" % t)
+                gate = keep.tile([P, S], F32, name="gate%d" % t)
+                diff = keep.tile([P, S], F32, name="diff%d" % t)
+                if t == 0:
+                    nc.scalar.activation(gate[:], s_sb[t][:].indirect(n4_t[:]), ACT.Sigmoid)
+                nc.scalar.activation(other[:], s_sb[t][:].indirect(n3_t[:]), ACT.Copy)
+                if t > 0:
+                    nc.scalar.activation(gate[:], s_sb[t][:].indirect(n4_t[:]), ACT.Sigmoid)
+                nc.vector.tensor_tensor(diff[:], s_sb[t][:, 0:S], other[:], ALU.subtract)
+                nc.vector.tensor_tensor(res[:, u, :], diff[:], gate[:], ALU.mult)
+                nc.sync.dma_start(out_rows[:, t, :], res[:, u, :])
+            nc.vector.tensor_copy(out_bf[:, :, 2 * half : 2 * half + 2], res[:].rearrange("p u j -> p j u"))
+
+        out_words = keep.tile([P, S], U32, name="out_words", align_bytes=64)
+        out_scales = keep.tile([P, S], U8, name="out_scales", align_bytes=64)
+        nc.vector.quantize_mx(
+            out=out_words[:].bitcast(FP8X4), scales=out_scales[:], in_=out_bf[:].rearrange("p j t -> p (j t)")
+        )
+        nc.sync.dma_start(out_1[0].rearrange("p c r -> p (c r)").bitcast(I32), out_words[:].bitcast(I32))
+        for q in range(4):
+            queue = nc.scalar if q % 2 == 0 else nc.sync
+            queue.dma_start(
+                out_2[0, 4 * q : 4 * q + 4, :].bitcast(I32), out_scales[32 * q : 32 * q + 4, :].bitcast(I32)
+            )

@@ -48,33 +48,38 @@ def tile_picked_hcandordergdif_none_po_kernel(
         place_scales = keep.tile([P, S], U8, name="place_scales", align_bytes=64)
         cand_words_dealt = keep.tile([P, C], U32, name="cand_words_dealt", align_bytes=64)
         cand_scales = keep.tile([P, C], U8, name="cand_scales", align_bytes=64)
-        cand_scales_dealt = keep.tile([P, C], U8, name="cand_scales_dealt", align_bytes=64)
+        cand_bytes_dealt = keep.tile([P, C], U8, name="cand_bytes_dealt", align_bytes=64)
 
-        nc.gpsimd.memset(w1_scales_raw[:].bitcast(I32), 0)
-        nc.gpsimd.memset(place_scales[:].bitcast(I32), 0)
-        nc.gpsimd.memset(cand_scales[:].bitcast(I32), 0)
+        warm_in = keep.tile([P, 1], F32, name="warm_in")
+        warm_out = keep.tile([P, 1], F32, name="warm_out")
+        nc.vector.memset(warm_in[:], 0.0)
+        nc.scalar.activation(warm_out[:], warm_in[:], ACT.Sigmoid)
+        nc.vector.memset(cand_scales[:].bitcast(I32), 0)
+        nc.vector.memset(place_scales[:].bitcast(I32), 0)
 
         nc.sync.dma_start(offs_t[:], offs)
-        nc.scalar.dma_start(w1_raw[:].bitcast(I32), w1_words[0].bitcast(I32))
-        nc.sync.dma_start(
+        nc.scalar.dma_start(
             table_scales[:].bitcast(I32), x_scales[0].bitcast(I32).unsqueeze(1).broadcast_to([16, 8, T // 4])
         )
+        nc.sync.dma_start(w1_raw[:].bitcast(I32), w1_words[0].bitcast(I32))
         for q in range(4):
-            nc.scalar.dma_start(
-                w1_scales_raw[32 * q : 32 * q + 4, :].bitcast(I32), w1_scales[0, 4 * q : 4 * q + 4, :].bitcast(I32)
+            queue = nc.scalar if q < 2 else nc.gpsimd
+            queue.dma_start(
+                w1_scales_raw[32 * q : 32 * q + 32, :].bitcast(I32),
+                w1_scales[0, 4 * q : 4 * q + 4, :].bitcast(I32).unsqueeze(0).broadcast_to([8, 4, H // 4]),
             )
-        nc.sync.dma_start(table_words[:].bitcast(I32), x_words[0].rearrange("p c r -> p (c r)").bitcast(I32))
         nc.sync.dma_start(n1_t[:], n1)
         nc.sync.dma_start(n2_t[:], n2)
+        nc.sync.dma_start(table_words[:].bitcast(I32), x_words[0].rearrange("p c r -> p (c r)").bitcast(I32))
         nc.sync.dma_start(cand_t[:], cand)
 
-        def place_scale_rows(dst, src, queues):
-            for j in range(4):
-                queues[j % len(queues)].dma_start(dst[j:P:32, :].bitcast(I32), src[8 * j : P : 32, :].bitcast(I32))
+        def move_scale_row(queue, dst, src, j):
+            queue.dma_start(dst[j:P:32, :].bitcast(I32), src[8 * j : P : 32, :].bitcast(I32))
 
         nc.vector.tensor_copy(place_bytes[:], table_scales[:].indirect(offs_t[:]))
-        place_scale_rows(place_scales, place_bytes, [nc.sync, nc.scalar])
-        nc.sync.dma_start(gs_t[:], gs.rearrange("(p t) o -> p (t o)", t=PACK))
+        for j in range(4):
+            move_scale_row(nc.scalar if j % 2 == 0 else nc.sync, place_scales, place_bytes, j)
+        nc.gpsimd.dma_start(gs_t[:], gs.rearrange("(p t) o -> p (t o)", t=PACK))
         nc.sync.dma_start(n3_t[:], n3)
         nc.sync.dma_start(n4_t[:], n4)
 
@@ -88,21 +93,28 @@ def tile_picked_hcandordergdif_none_po_kernel(
         )
         nc.vector.tensor_copy(place_words[:], table_words[:].indirect(offs_t[:]))
 
-        y_sb, larger, smaller = [], [], []
-        for t in range(PACK):
-            y_ps = psum.tile([P, S], F32, name="y_ps", tag="bank%d" % t)
+        halves = [slice(0, S // 2), slice(S // 2, S)]
+        whole = slice(0, S)
+        y_sb = [keep.tile([P, S], F32, name="y%d" % t) for t in range(PACK)]
+        larger, smaller = [], []
+
+        def project(t, cols, bank):
+            y_ps = psum.tile([P, cols.stop - cols.start], F32, name="y_ps", tag=bank)
             nc.tensor.matmul_mx(
                 out=y_ps[:],
                 lhsT=w1_dealt[:, 2 * P * t : 2 * P * (t + 1)].bitcast(FP4X4),
                 lhsT_scale=w1_scales_dealt[:, P * t : P * (t + 1)],
-                rhs=place_words[:].bitcast(FP8X4),
-                rhs_scale=place_scales[:],
+                rhs=place_words[:, cols].bitcast(FP8X4),
+                rhs_scale=place_scales[:, cols],
                 start=True,
                 stop=True,
             )
-            y_t = keep.tile([P, S], F32, name="y%d" % t)
-            nc.vector.tensor_copy(y_t[:], y_ps[:])
-            y_sb.append(y_t)
+            return y_ps
+
+        nc.vector.tensor_copy(y_sb[0][:, halves[0]], project(0, halves[0], "bank0")[:])
+        nc.scalar.activation(y_sb[0][:, halves[1]], project(0, halves[1], "bank4")[:], ACT.Copy)
+        for t in range(1, PACK):
+            nc.vector.tensor_copy(y_sb[t][:], project(t, whole, "bank%d" % t)[:])
 
         z_bf = keep.tile([P, S, PACK], BF16, name="z_bf", align_bytes=64)
 
@@ -120,16 +132,17 @@ def tile_picked_hcandordergdif_none_po_kernel(
 
         cand_bytes = keep.tile([P, C], U8, name="cand_bytes", tag="pa1", align_bytes=64)
         nc.vector.tensor_copy(cand_bytes[:], table_scales[:].indirect(cand_t[:]))
-        place_scale_rows(cand_scales, cand_bytes, [nc.sync])
+        nc.vector.tensor_copy(
+            cand_bytes_dealt[:].rearrange("p (t m) -> p t m", t=PACK),
+            cand_bytes[:].rearrange("p (m t) -> p t m", t=PACK),
+        )
+        for j in range(4):
+            move_scale_row(nc.sync, cand_scales, cand_bytes_dealt, j)
         cand_words = keep.tile([P, C], U32, name="cand_words", tag="pa3", align_bytes=64)
         nc.vector.tensor_copy(cand_words[:], table_words[:].indirect(cand_t[:]))
         nc.vector.tensor_copy(
             cand_words_dealt[:].bitcast(I32).rearrange("p (t m) -> p t m", t=PACK),
             cand_words[:].bitcast(I32).rearrange("p (m t) -> p t m", t=PACK),
-        )
-        nc.vector.tensor_copy(
-            cand_scales_dealt[:].rearrange("p (t m) -> p t m", t=PACK),
-            cand_scales[:].rearrange("p (m t) -> p t m", t=PACK),
         )
 
         dt = [keep.tile([P, S], F32, name="dt%d" % t) for t in range(PACK)]
@@ -138,7 +151,6 @@ def tile_picked_hcandordergdif_none_po_kernel(
                 nc.scalar.activation(dt[t][:].indirect(n1_t[:]), larger[t][:], ACT.Copy)
             for t in (2 * pair, 2 * pair + 1):
                 nc.scalar.activation(dt[t][:].indirect(n2_t[:]), smaller[t][:], ACT.Copy)
-        halves = [slice(0, S // 2), slice(S // 2, S)]
         for t in range(PACK - 1):
             nc.vector.tensor_scalar(z_bf[:, :, t], dt[t][:], gs_t[:, t : t + 1], None, ALU.mult)
         last = PACK - 1
@@ -161,46 +173,58 @@ def tile_picked_hcandordergdif_none_po_kernel(
             nc.tensor.matmul_mx(
                 out=s_ps[:],
                 lhsT=cand_words_dealt[:, P * t : P * (t + 1)].bitcast(FP8X4),
-                lhsT_scale=cand_scales_dealt[:, P * t : P * (t + 1)],
+                lhsT_scale=cand_scales[:, P * t : P * (t + 1)],
                 rhs=z_words[:, cols].bitcast(FP8X4),
                 rhs_scale=z_scales[:, cols],
                 start=True,
                 stop=True,
             )
-            nc.vector.tensor_scalar(s_sb[t][:, cols], s_ps[:], 0.0625, None, ALU.mult)
+            return s_ps
 
-        score(0, halves[0], "bank0")
-        score(0, halves[1], "bank4")
-        for t in range(1, PACK):
-            score(t, slice(0, S), "bank%d" % (4 + t))
+        nc.vector.tensor_scalar(s_sb[0][:, halves[0]], score(0, halves[0], "bank5")[:], 0.0625, None, ALU.mult)
+        nc.scalar.activation(s_sb[0][:, halves[1]], score(0, halves[1], "bank6")[:], ACT.Copy, scale=0.0625)
+        for t, bank in ((1, "bank7"), (2, "bank0"), (3, "bank4")):
+            nc.vector.tensor_scalar(s_sb[t][:, whole], score(t, whole, bank)[:], 0.0625, None, ALU.mult)
 
         out_rows = out_0.rearrange("(p t) j -> p t j", t=PACK)
         out_bf = keep.tile([P, S, PACK], BF16, name="out_bf", align_bytes=64)
-        for half in range(2):
-            res = keep.tile([P, 2, S], F32, name="res%d" % half)
-            for u in range(2):
-                t = 2 * half + u
-                other = keep.tile([P, S], F32, name="other%d" % t)
-                gate = keep.tile([P, S], F32, name="gate%d" % t)
-                diff = keep.tile([P, S], F32, name="diff%d" % t)
-                if t == 0:
-                    nc.scalar.activation(gate[:], s_sb[t][:].indirect(n4_t[:]), ACT.Sigmoid)
-                nc.scalar.activation(other[:], s_sb[t][:].indirect(n3_t[:]), ACT.Copy)
-                if t > 0:
-                    nc.scalar.activation(gate[:], s_sb[t][:].indirect(n4_t[:]), ACT.Sigmoid)
-                nc.vector.tensor_tensor(diff[:], s_sb[t][:, 0:S], other[:], ALU.subtract)
-                nc.vector.tensor_tensor(res[:, u, :], diff[:], gate[:], ALU.mult)
-                nc.sync.dma_start(out_rows[:, t, :], res[:, u, :])
-            nc.vector.tensor_copy(out_bf[:, :, 2 * half : 2 * half + 2], res[:].rearrange("p u j -> p j u"))
-
         out_words = keep.tile([P, S], U32, name="out_words", align_bytes=64)
         out_scales = keep.tile([P, S], U8, name="out_scales", align_bytes=64)
-        nc.vector.quantize_mx(
-            out=out_words[:].bitcast(FP8X4), scales=out_scales[:], in_=out_bf[:].rearrange("p j t -> p (j t)")
-        )
-        nc.sync.dma_start(out_1[0].rearrange("p c r -> p (c r)").bitcast(I32), out_words[:].bitcast(I32))
+        res = [keep.tile([P, 2, S], F32, name="res%d" % pair) for pair in range(2)]
+
+        def finish(t, cols):
+            width = cols.stop - cols.start
+            entries = slice(cols.start // 16, cols.stop // 16)
+            other = keep.tile([P, width], F32, name="other%d_%d" % (t, cols.start))
+            gate = keep.tile([P, width], F32, name="gate%d_%d" % (t, cols.start))
+            diff = keep.tile([P, width], F32, name="diff%d_%d" % (t, cols.start))
+            nc.scalar.activation(other[:], s_sb[t][:].indirect(n3_t[:, entries]), ACT.Copy)
+            nc.scalar.activation(gate[:], s_sb[t][:].indirect(n4_t[:, entries]), ACT.Sigmoid)
+            nc.vector.tensor_tensor(diff[:], s_sb[t][:, cols], other[:], ALU.subtract)
+            nc.vector.tensor_tensor(res[t // 2][:, t % 2, cols], diff[:], gate[:], ALU.mult)
+            nc.sync.dma_start(out_rows[:, t, cols], res[t // 2][:, t % 2, cols])
+
+        def round_pair(pair, cols):
+            nc.vector.tensor_copy(
+                out_bf[:, cols, 2 * pair : 2 * pair + 2], res[pair][:, :, cols].rearrange("p u j -> p j u")
+            )
+
+        finish(0, whole)
+        finish(1, whole)
+        round_pair(0, whole)
+        finish(2, whole)
+        words_out = out_1[0].rearrange("p c r -> p (c r)").bitcast(I32)
+        for cols in halves:
+            finish(3, cols)
+            round_pair(1, cols)
+            nc.vector.quantize_mx(
+                out=out_words[:, cols].bitcast(FP8X4),
+                scales=out_scales[:, cols],
+                in_=out_bf[:, cols, :].rearrange("p j t -> p (j t)"),
+            )
+            nc.sync.dma_start(words_out[:, cols], out_words[:, cols].bitcast(I32))
         for q in range(4):
-            queue = nc.scalar if q % 2 == 0 else nc.sync
+            queue = nc.sync if q == 3 else nc.scalar
             queue.dma_start(
                 out_2[0, 4 * q : 4 * q + 4, :].bitcast(I32), out_scales[32 * q : 32 * q + 4, :].bitcast(I32)
             )

@@ -63,15 +63,14 @@ def tile_picked_hcandordergdif_none_po_kernel(
         )
         nc.sync.dma_start(w1_raw[:].bitcast(I32), w1_words[0].bitcast(I32))
         for q in range(4):
-            queue = nc.scalar if q < 2 else nc.gpsimd
+            queue = nc.scalar if q < 2 else nc.sync
             queue.dma_start(
                 w1_scales_raw[32 * q : 32 * q + 32, :].bitcast(I32),
                 w1_scales[0, 4 * q : 4 * q + 4, :].bitcast(I32).unsqueeze(0).broadcast_to([8, 4, H // 4]),
             )
+        nc.sync.dma_start(table_words[:].bitcast(I32), x_words[0].rearrange("p c r -> p (c r)").bitcast(I32))
         nc.sync.dma_start(n1_t[:], n1)
         nc.sync.dma_start(n2_t[:], n2)
-        nc.sync.dma_start(table_words[:].bitcast(I32), x_words[0].rearrange("p c r -> p (c r)").bitcast(I32))
-        nc.sync.dma_start(cand_t[:], cand)
 
         def move_scale_row(queue, dst, src, j):
             queue.dma_start(dst[j:P:32, :].bitcast(I32), src[8 * j : P : 32, :].bitcast(I32))
@@ -79,9 +78,10 @@ def tile_picked_hcandordergdif_none_po_kernel(
         nc.vector.tensor_copy(place_bytes[:], table_scales[:].indirect(offs_t[:]))
         for j in range(4):
             move_scale_row(nc.scalar if j % 2 == 0 else nc.sync, place_scales, place_bytes, j)
-        nc.gpsimd.dma_start(gs_t[:], gs.rearrange("(p t) o -> p (t o)", t=PACK))
+        nc.sync.dma_start(cand_t[:], cand)
         nc.sync.dma_start(n3_t[:], n3)
         nc.sync.dma_start(n4_t[:], n4)
+        nc.sync.dma_start(gs_t[:], gs.rearrange("(p t) o -> p (t o)", t=PACK))
 
         nc.vector.tensor_copy(
             w1_dealt[:].rearrange("p (t m b) -> p t m b", t=PACK, b=2),
@@ -192,37 +192,42 @@ def tile_picked_hcandordergdif_none_po_kernel(
         out_scales = keep.tile([P, S], U8, name="out_scales", align_bytes=64)
         res = [keep.tile([P, 2, S], F32, name="res%d" % pair) for pair in range(2)]
 
-        def finish(t, cols):
-            width = cols.stop - cols.start
+        def difference(t):
+            other = keep.tile([P, S], F32, name="other%d" % t)
+            diff = keep.tile([P, S], F32, name="diff%d" % t)
+            nc.scalar.activation(other[:], s_sb[t][:].indirect(n3_t[:]), ACT.Copy)
+            nc.vector.tensor_tensor(diff[:], s_sb[t][:, whole], other[:], ALU.subtract)
+            return diff
+
+        def gated(t, diff, cols):
+            gate = keep.tile([P, cols.stop - cols.start], F32, name="gate%d_%d" % (t, cols.start))
             entries = slice(cols.start // 16, cols.stop // 16)
-            other = keep.tile([P, width], F32, name="other%d_%d" % (t, cols.start))
-            gate = keep.tile([P, width], F32, name="gate%d_%d" % (t, cols.start))
-            diff = keep.tile([P, width], F32, name="diff%d_%d" % (t, cols.start))
-            nc.scalar.activation(other[:], s_sb[t][:].indirect(n3_t[:, entries]), ACT.Copy)
             nc.scalar.activation(gate[:], s_sb[t][:].indirect(n4_t[:, entries]), ACT.Sigmoid)
-            nc.vector.tensor_tensor(diff[:], s_sb[t][:, cols], other[:], ALU.subtract)
-            nc.vector.tensor_tensor(res[t // 2][:, t % 2, cols], diff[:], gate[:], ALU.mult)
-            nc.sync.dma_start(out_rows[:, t, cols], res[t // 2][:, t % 2, cols])
+            nc.vector.tensor_tensor(res[t // 2][:, t % 2, cols], diff[:, cols], gate[:], ALU.mult)
 
         def round_pair(pair, cols):
             nc.vector.tensor_copy(
                 out_bf[:, cols, 2 * pair : 2 * pair + 2], res[pair][:, :, cols].rearrange("p u j -> p j u")
             )
 
-        finish(0, whole)
-        finish(1, whole)
-        round_pair(0, whole)
-        finish(2, whole)
-        words_out = out_1[0].rearrange("p c r -> p (c r)").bitcast(I32)
+        for t in range(last):
+            gated(t, difference(t), whole)
+            nc.sync.dma_start(out_rows[:, t, :], res[t // 2][:, t % 2, :])
+            if t == 1:
+                round_pair(0, whole)
+        diff_last = difference(last)
         for cols in halves:
-            finish(3, cols)
+            gated(last, diff_last, cols)
+        nc.sync.dma_start(out_rows[:, last, :], res[1][:, 1, :])
+        for cols in halves:
             round_pair(1, cols)
+        for cols in halves:
             nc.vector.quantize_mx(
                 out=out_words[:, cols].bitcast(FP8X4),
                 scales=out_scales[:, cols],
                 in_=out_bf[:, cols, :].rearrange("p j t -> p (j t)"),
             )
-            nc.sync.dma_start(words_out[:, cols], out_words[:, cols].bitcast(I32))
+        nc.sync.dma_start(out_1[0].rearrange("p c r -> p (c r)").bitcast(I32), out_words[:].bitcast(I32))
         for q in range(4):
             queue = nc.sync if q == 3 else nc.scalar
             queue.dma_start(

from contextlib import ExitStack

import concourse.mybir as mybir

K, T, S, H, W, C = 512, 2048, 256, 512, 128, 512
FLOPS = 2 * K * H * S + 2 * K * C * S

F32 = mybir.dt.float32
BF16 = mybir.dt.bfloat16
I32 = mybir.dt.int32
U32 = mybir.dt.uint32
U16 = mybir.dt.uint16
U8 = mybir.dt.uint8
FP8X4 = mybir.dt.float8_e4m3fn_x4
FP4X4 = mybir.dt.float4_e2m1fn_x4
ALU = mybir.AluOpType
ACT = mybir.ActivationFunctionType

P = 128
PACK = 4


def tile_picked_hcandordergdif_none_po_kernel(
    tc, x_words, x_scales, w1_words, w1_scales, gs, offs, n1, n2, cand, n3, n4, out_0, out_1, out_2
):
    nc = tc.nc
    with ExitStack() as ctx:
        lists = ctx.enter_context(tc.tile_pool(name="lists", bufs=1))
        keep = ctx.enter_context(tc.tile_pool(name="keep", bufs=1))
        psum = ctx.enter_context(tc.psum_pool(name="psum", bufs=1))

        offs_t = lists.tile([P, S // 16], U16, name="offs_t")
        cand_t = lists.tile([P, C // 16], U16, name="cand_t")
        n1_t = lists.tile([P, W // 16], U16, name="n1_t")
        n2_t = lists.tile([P, W // 16], U16, name="n2_t")
        n3_t = lists.tile([P, S // 16], U16, name="n3_t")
        n4_t = lists.tile([P, S // 16], U16, name="n4_t")

        table_words = keep.tile([P, T], U32, name="table_words", align_bytes=64)
        table_scales = keep.tile([P, T], U8, name="table_scales", align_bytes=64)
        w1_raw = keep.tile([P, 2 * H], U8, name="w1_raw", align_bytes=64)
        w1_scales_raw = keep.tile([P, H], U8, name="w1_scales_raw", align_bytes=64)
        w1_dealt = keep.tile([P, 2 * H], U8, name="w1_dealt", align_bytes=64)
        w1_scales_dealt = keep.tile([P, H], U8, name="w1_scales_dealt", align_bytes=64)
        gs_t = keep.tile([P, PACK], F32, name="gs_t")
        place_words = keep.tile([P, S], U32, name="place_words", align_bytes=64)
        place_bytes = keep.tile([P, S], U8, name="place_bytes", align_bytes=64)
        place_scales = keep.tile([P, S], U8, name="place_scales", align_bytes=64)
        cand_words_dealt = keep.tile([P, C], U32, name="cand_words_dealt", align_bytes=64)
        cand_scales = keep.tile([P, C], U8, name="cand_scales", align_bytes=64)
        cand_bytes_dealt = keep.tile([P, C], U8, name="cand_bytes_dealt", align_bytes=64)

        warm_in = keep.tile([P, 1], F32, name="warm_in")
        warm_out = keep.tile([P, 1], F32, name="warm_out")
        nc.vector.memset(warm_in[:], 0.0)
        nc.scalar.activation(warm_out[:], warm_in[:], ACT.Sigmoid)
        nc.vector.memset(cand_scales[:].bitcast(I32), 0)
        nc.vector.memset(place_scales[:].bitcast(I32), 0)

        nc.sync.dma_start(offs_t[:], offs)
        nc.scalar.dma_start(
            table_scales[:].bitcast(I32), x_scales[0].bitcast(I32).unsqueeze(1).broadcast_to([16, 8, T // 4])
        )
        nc.sync.dma_start(w1_raw[:].bitcast(I32), w1_words[0].bitcast(I32))
        for q in range(4):
            queue = nc.scalar if q < 2 else nc.sync
            queue.dma_start(
                w1_scales_raw[32 * q : 32 * q + 32, :].bitcast(I32),
                w1_scales[0, 4 * q : 4 * q + 4, :].bitcast(I32).unsqueeze(0).broadcast_to([8, 4, H // 4]),
            )
        nc.sync.dma_start(table_words[:].bitcast(I32), x_words[0].rearrange("p c r -> p (c r)").bitcast(I32))
        nc.sync.dma_start(n1_t[:], n1)
        nc.sync.dma_start(n2_t[:], n2)

        def move_scale_row(queue, dst, src, j):
            queue.dma_start(dst[j:P:32, :].bitcast(I32), src[8 * j : P : 32, :].bitcast(I32))

        nc.vector.tensor_copy(place_bytes[:], table_scales[:].indirect(offs_t[:]))
        for j in range(4):
            move_scale_row(nc.scalar if j % 2 == 0 else nc.sync, place_scales, place_bytes, j)
        nc.sync.dma_start(cand_t[:], cand)
        nc.sync.dma_start(n3_t[:], n3)
        nc.sync.dma_start(n4_t[:], n4)
        nc.sync.dma_start(gs_t[:], gs.rearrange("(p t) o -> p (t o)", t=PACK))

        nc.vector.tensor_copy(
            w1_dealt[:].rearrange("p (t m b) -> p t m b", t=PACK, b=2),
            w1_raw[:].rearrange("p (m t b) -> p t m b", t=PACK, b=2),
        )
        nc.vector.tensor_copy(
            w1_scales_dealt[:].rearrange("p (t m) -> p t m", t=PACK),
            w1_scales_raw[:].rearrange("p (m t) -> p t m", t=PACK),
        )
        nc.vector.tensor_copy(place_words[:], table_words[:].indirect(offs_t[:]))

        halves = [slice(0, S // 2), slice(S // 2, S)]
        whole = slice(0, S)
        y_sb = [keep.tile([P, S], F32, name="y%d" % t) for t in range(PACK)]
        larger, smaller = [], []

        def project(t, cols, bank):
            y_ps = psum.tile([P, cols.stop - cols.start], F32, name="y_ps", tag=bank)
            nc.tensor.matmul_mx(
                out=y_ps[:],
                lhsT=w1_dealt[:, 2 * P * t : 2 * P * (t + 1)].bitcast(FP4X4),
                lhsT_scale=w1_scales_dealt[:, P * t : P * (t + 1)],
                rhs=place_words[:, cols].bitcast(FP8X4),
                rhs_scale=place_scales[:, cols],
                start=True,
                stop=True,
            )
            return y_ps

        nc.vector.tensor_copy(y_sb[0][:, halves[0]], project(0, halves[0], "bank0")[:])
        nc.scalar.activation(y_sb[0][:, halves[1]], project(0, halves[1], "bank4")[:], ACT.Copy)
        for t in range(1, PACK):
            nc.vector.tensor_copy(y_sb[t][:], project(t, whole, "bank%d" % t)[:])

        z_bf = keep.tile([P, S, PACK], BF16, name="z_bf", align_bytes=64)

        for t in range(PACK):
            pa = keep.tile([P, W], F32, name="pa%d" % t, tag="pa%d" % t, align_bytes=64)
            pb = keep.tile([P, W], F32, name="pb%d" % t)
            nc.scalar.activation(pa[:], y_sb[t][:].indirect(n1_t[:]), ACT.Copy)
            nc.scalar.activation(pb[:], y_sb[t][:].indirect(n2_t[:]), ACT.Copy)
            ra = keep.tile([P, W], F32, name="ra%d" % t)
            rb = keep.tile([P, W], F32, name="rb%d" % t)
            nc.vector.tensor_tensor(ra[:], pa[:], pb[:], ALU.max)
            nc.vector.tensor_tensor(rb[:], pa[:], pb[:], ALU.min)
            larger.append(ra)
            smaller.append(rb)

        cand_bytes = keep.tile([P, C], U8, name="cand_bytes", tag="pa1", align_bytes=64)
        nc.vector.tensor_copy(cand_bytes[:], table_scales[:].indirect(cand_t[:]))
        nc.vector.tensor_copy(
            cand_bytes_dealt[:].rearrange("p (t m) -> p t m", t=PACK),
            cand_bytes[:].rearrange("p (m t) -> p t m", t=PACK),
        )
        for j in range(4):
            move_scale_row(nc.sync, cand_scales, cand_bytes_dealt, j)
        cand_words = keep.tile([P, C], U32, name="cand_words", tag="pa3", align_bytes=64)
        nc.vector.tensor_copy(cand_words[:], table_words[:].indirect(cand_t[:]))
        nc.vector.tensor_copy(
            cand_words_dealt[:].bitcast(I32).rearrange("p (t m) -> p t m", t=PACK),
            cand_words[:].bitcast(I32).rearrange("p (m t) -> p t m", t=PACK),
        )

        dt = [keep.tile([P, S], F32, name="dt%d" % t) for t in range(PACK)]
        for pair in range(2):
            for t in (2 * pair, 2 * pair + 1):
                nc.scalar.activation(dt[t][:].indirect(n1_t[:]), larger[t][:], ACT.Copy)
            for t in (2 * pair, 2 * pair + 1):
                nc.scalar.activation(dt[t][:].indirect(n2_t[:]), smaller[t][:], ACT.Copy)
        for t in range(PACK - 1):
            nc.vector.tensor_scalar(z_bf[:, :, t], dt[t][:], gs_t[:, t : t + 1], None, ALU.mult)
        last = PACK - 1
        for cols in halves:
            nc.vector.tensor_scalar(z_bf[:, cols, last], dt[last][:, cols], gs_t[:, last:PACK], None, ALU.mult)

        z_words = keep.tile([P, S], U32, name="z_words", align_bytes=64)
        z_scales = keep.tile([P, S], U8, name="z_scales", align_bytes=64)
        for cols in halves:
            nc.vector.quantize_mx(
                out=z_words[:, cols].bitcast(FP8X4),
                scales=z_scales[:, cols],
                in_=z_bf[:, cols, :].rearrange("p j t -> p (j t)"),
            )

        s_sb = [keep.tile([P, 2 * S], F32, name="s%d" % t) for t in range(PACK)]

        def score(t, cols, bank):
            s_ps = psum.tile([P, cols.stop - cols.start], F32, name="s_ps", tag=bank)
            nc.tensor.matmul_mx(
                out=s_ps[:],
                lhsT=cand_words_dealt[:, P * t : P * (t + 1)].bitcast(FP8X4),
                lhsT_scale=cand_scales[:, P * t : P * (t + 1)],
                rhs=z_words[:, cols].bitcast(FP8X4),
                rhs_scale=z_scales[:, cols],
                start=True,
                stop=True,
            )
            return s_ps

        nc.vector.tensor_scalar(s_sb[0][:, halves[0]], score(0, halves[0], "bank5")[:], 0.0625, None, ALU.mult)
        nc.scalar.activation(s_sb[0][:, halves[1]], score(0, halves[1], "bank6")[:], ACT.Copy, scale=0.0625)
        for t, bank in ((1, "bank7"), (2, "bank0"), (3, "bank4")):
            nc.vector.tensor_scalar(s_sb[t][:, whole], score(t, whole, bank)[:], 0.0625, None, ALU.mult)

        out_rows = out_0.rearrange("(p t) j -> p t j", t=PACK)
        out_bf = keep.tile([P, S, PACK], BF16, name="out_bf", align_bytes=64)
        out_words = keep.tile([P, S], U32, name="out_words", align_bytes=64)
        out_scales = keep.tile([P, S], U8, name="out_scales", align_bytes=64)
        res = [keep.tile([P, 2, S], F32, name="res%d" % pair) for pair in range(2)]

        def difference(t):
            other = keep.tile([P, S], F32, name="other%d" % t)
            diff = keep.tile([P, S], F32, name="diff%d" % t)
            nc.scalar.activation(other[:], s_sb[t][:].indirect(n3_t[:]), ACT.Copy)
            nc.vector.tensor_tensor(diff[:], s_sb[t][:, whole], other[:], ALU.subtract)
            return diff

        def gated(t, diff, cols):
            gate = keep.tile([P, cols.stop - cols.start], F32, name="gate%d_%d" % (t, cols.start))
            entries = slice(cols.start // 16, cols.stop // 16)
            nc.scalar.activation(gate[:], s_sb[t][:].indirect(n4_t[:, entries]), ACT.Sigmoid)
            nc.vector.tensor_tensor(res[t // 2][:, t % 2, cols], diff[:, cols], gate[:], ALU.mult)

        def round_pair(pair, cols):
            nc.vector.tensor_copy(
                out_bf[:, cols, 2 * pair : 2 * pair + 2], res[pair][:, :, cols].rearrange("p u j -> p j u")
            )

        for t in range(last):
            gated(t, difference(t), whole)
            nc.sync.dma_start(out_rows[:, t, :], res[t // 2][:, t % 2, :])
            if t == 1:
                round_pair(0, whole)
        diff_last = difference(last)
        for cols in halves:
            gated(last, diff_last, cols)
        nc.sync.dma_start(out_rows[:, last, :], res[1][:, 1, :])
        for cols in halves:
            round_pair(1, cols)
        for cols in halves:
            nc.vector.quantize_mx(
                out=out_words[:, cols].bitcast(FP8X4),
                scales=out_scales[:, cols],
                in_=out_bf[:, cols, :].rearrange("p j t -> p (j t)"),
            )
        nc.sync.dma_start(out_1[0].rearrange("p c r -> p (c r)").bitcast(I32), out_words[:].bitcast(I32))
        for q in range(4):
            queue = nc.sync if q == 3 else nc.scalar
            queue.dma_start(
                out_2[0, 4 * q : 4 * q + 4, :].bitcast(I32), out_scales[32 * q : 32 * q + 4, :].bitcast(I32)
            )
